import numpy as np, ml_dtypes
CORES = [65,66,69,71,193,194,197,199,321,322,325,327,449,450,453,455]
N = 16
B, S = 16, 64
CAPP = 2
def entries(a): return a.T.reshape(-1)
def pack(v, P): return np.ascontiguousarray(np.asarray(v, np.int32).reshape(-1, P).T)
def lists(rng, how):
    Q = rng.integers(0, N * B, N * B)
    O = np.stack([rng.permutation(np.repeat(rng.permutation(N)[:B // CAPP], CAPP)) if how == "full" else rng.permutation(np.repeat(np.arange(N), CAPP))[:B] for r in range(N)])
    Q = (B * O + Q.reshape(N, B) % B).reshape(-1)
    if how == "alike": Q = (B * O + rng.integers(B)).reshape(-1)
    if how == "edge": Q = (B * O + np.where(rng.random((N, B)) < 0.5, 0, B - 1)).reshape(-1)
    if how == "full": Q = (B * O + (rng.integers(B) + np.stack([np.array([np.sum(O[r, :i] == O[r, i]) for i in range(B)]) for r in range(N)])) % B).reshape(-1)
    if how == "sorted": Q = np.sort(Q.reshape(N, B), axis=1).reshape(-1)
    return {"parent": np.broadcast_to(pack(Q, 16), (N, 16, N * B // 16)).copy()}
def setup_inputs(rng):
    return dict({"c": rng.standard_normal((N, 128, B * S), dtype=np.float32).astype(ml_dtypes.bfloat16)}, **lists(rng, "uniform"))
def setup_inputs_alike(rng):
    d = setup_inputs(rng); d.update(lists(rng, "alike"))
    for k in ("c",): d[k] = (d[k].astype(np.float32) * 1048576.0).astype(d[k].dtype)
    return d
def setup_inputs_edge(rng):
    d = setup_inputs(rng); d.update(lists(rng, "edge"))
    for k in ("c",): d[k] = (d[k].astype(np.float32) * (1 / 1024.0)).astype(d[k].dtype)
    return d
def setup_inputs_full(rng):
    d = setup_inputs(rng); d.update(lists(rng, "full"))
    return d
def setup_inputs_sorted(rng):
    d = setup_inputs(rng); d.update(lists(rng, "sorted"))
    return d
def check_inputs(x):
    bad = []
    if x["parent"].min() < 0 or x["parent"].max() >= N * B: bad.append("parent out of range")
    if not all(np.array_equal(a, x["parent"][0]) for a in x["parent"]): bad.append("parent isn't alike on all ranks")
    if max(int(np.bincount(q // B, minlength=N).max()) for q in entries(x["parent"][0]).reshape(N, B)) > CAPP: bad.append("more than CAPP beams of a rank have their parents on one rank")
    return bad
def reference(c, parent):
    A = np.concatenate(list(c), axis=1).reshape(128, N * B, S)
    Y = A[:, entries(parent[0]), :]
    return {"y": np.stack([Y[:, B * r:B * r + B].reshape(128, B * S) for r in range(N)])}

@@ -1,0 +1,250 @@
+from concourse.bass import DstId, RemoteDMATransfer
+from concourse.mybir import AluOpType, AxisListType
+
+SCRATCH = {
+    "cbuf": ("sbuf", [128, 1024], "bfloat16"),
+    "pack": ("sbuf", [128, 2048], "bfloat16"),
+    "land": ("sbuf", [128, 2048], "bfloat16"),
+    "rbuf": ("sbuf", [128, 512], "bfloat16"),
+    "ybuf": ("sbuf", [128, 1024], "bfloat16"),
+    "par2": ("sbuf", [128, 32], "int32"),
+    "cn": ("sbuf", [128, 32], "int32"),
+    "sg": ("sbuf", [128, 32], "int32"),
+    "eb": ("sbuf", [128, 32], "int32"),
+    "vb": ("sbuf", [128, 32], "int32"),
+    "pre": ("sbuf", [128, 32], "float32"),
+    "ft": ("sbuf", [128, 32], "float32"),
+    "red": ("sbuf", [128, 1], "float32"),
+    "dl": ("sbuf", [128, 1], "float32"),
+    "ones": ("sbuf", [128, 128], "bfloat16"),
+    "s64": ("sbuf", [128, 128], "bfloat16"),
+    "es": ("sbuf", [128, 128], "bfloat16"),
+    "e16": ("sbuf", [128, 64], "bfloat16"),
+    "l2": ("sbuf", [128, 128], "bfloat16"),
+    "cc": ("sbuf", [128, 128], "bfloat16"),
+    "qi": ("sbuf", [128, 1], "int32"),
+    "qa": ("sbuf", [128, 1], "int32"),
+    "qm": ("sbuf", [128, 1], "float32"),
+    "offs": ("sbuf", [128, 128], "uint16"),
+    "offr": ("sbuf", [128, 64], "uint16"),
+    "parf": ("sbuf", [128, 1], "float32"),
+    "lo": ("sbuf", [128, 1], "int32"),
+    "lof": ("sbuf", [128, 1], "float32"),
+    "lo8": ("sbuf", [128, 1], "float32"),
+    "dg": ("sbuf", [128, 64], "bfloat16"),
+    "am": ("sbuf", [128, 64], "float32"),
+    "bm": ("sbuf", [128, 64], "float32"),
+    "dm": ("sbuf", [128, 64], "float32"),
+    "ks": ("sbuf", [128, 1], "float32"),
+    "pos": ("sbuf", [128, 1], "float32"),
+    "lr": ("sbuf", [128, 128], "bfloat16"),
+    "pss": ("psum", [128, 512], "float32"),
+    "psm": ("psum", [128, 512], "float32"),
+    "psr": ("psum", [128, 512], "float32"),
+}
+SEMAPHORES = ["arr", "rin", "snt"] + ["q%d" % i for i in range(64)]
+
+W = 128
+A = AluOpType
+
+
+def rank_program(g, core, T, topo):
+    rank = T.rank_of(core)
+    if rank is None:
+        return
+    V, PE, SY, AC = g.vector, g.tensor, g.sync, g.scalar
+    pool = [0]
+
+    def tok(instr, n=1):
+        s = T.sem["q%d" % pool[0]]
+        pool[0] += 1
+        instr.then_inc(s, n)
+        return (s, n)
+
+    def need(q, *toks):
+        for s, n in toks:
+            q.wait_ge(s, n)
+
+    cores = list(T.cores)
+    byhost = {}
+    for x in cores:
+        byhost.setdefault(topo.host(x), []).append(x)
+
+    def kinds(x):
+        sw = cb = dgn = None
+        for h, lst in byhost.items():
+            if h == topo.host(x):
+                continue
+            if not topo.may_write(x, lst[0]):
+                dgn = h
+            elif topo.same_plane(x, lst[0]):
+                sw = h
+            else:
+                cb = h
+        return sw, cb, dgn
+
+    def relay_of(x):
+        sw, cb, _ = kinds(x)
+        mine = byhost[topo.host(x)]
+        samedie = [z for z in mine if topo.die(z) == topo.die(x)]
+        via = sw if samedie.index(x) % 2 == 0 else cb
+        return byhost[via][mine.index(x)]
+
+    def bits(m):
+        return [e for e in range(16) if (m >> e) & 1]
+
+    def msk(es):
+        m = 0
+        for e in es:
+            m |= 1 << e
+        return m
+
+    def did(d):
+        rid, pid = topo.addr(d, core)
+        return DstId(rid=rid, pnc=pid)
+
+    sw, cb, dgn = kinds(core)
+    mine = byhost[topo.host(core)]
+    peers = [x for x in mine if x != core]
+    eo = bits(topo.mask(core, byhost[sw][0]))
+    eon = [e for e in bits(topo.mask(core, peers[0])) if e not in eo]
+    base = {h: min(T.rank_of(x) for x in lst) for h, lst in byhost.items()}
+
+    t_c = tok(SY.dma_start(T.cbuf[:, :], T.c[:, :]), 16)
+    t_pa = tok(AC.dma_start(T.par2[0:16, 0:16], T.parent[:, :]), 16)
+    t_pb = tok(AC.dma_start(T.par2[0:16, 16:32], T.parent[:, :]), 16)
+
+    t_qi = tok(g.iota(T.qi[:, 0:1], [[0, 1]], 0, 1))
+    t_cc = tok(g.iota(T.cc[0:1, 0:128], [[0, 32], [16, 4]], 0, 0, allow_small_or_imprecise_dtypes=True))
+
+    t_s64a = tok(V.memset(T.s64[0:32, 0:128], -64.0))
+    t_dla = tok(V.memset(T.dl[0:32, 0:1], -15.0))
+    t_ones = tok(V.memset(T.ones[0:32, 0:128], 1.0))
+    need(V, t_s64a, t_dla)
+    t_s64 = tok(V.memset(T.s64[0:16, 0:128], 64.0))
+    t_dl = tok(V.memset(T.dl[0:16, 0:1], 255.0))
+    t_cn0 = tok(V.memset(T.cn[0:16, 0:16], 16 * rank + 255))
+    t_cn1 = tok(V.memset(T.cn[0:16, 16:32], 16 * rank + 15))
+    t_sg0 = tok(V.memset(T.sg[0:16, 0:16], -1))
+    t_sg1 = tok(V.memset(T.sg[0:16, 16:32], 1))
+    t_pr0 = tok(V.memset(T.pre[0:32, 0:16], -240.0))
+    t_pr1 = tok(V.memset(T.pre[0:32, 16:32], 15.0))
+    need(V, t_qi)
+    t_qa = tok(V.tensor_scalar(T.qa[:, 0:1], T.qi[:, 0:1], 15, None, A.bitwise_and))
+    need(V, t_qa)
+    t_qm = tok(V.tensor_copy(T.qm[:, 0:1], T.qa[:, 0:1]))
+
+    need(g, t_s64)
+    t_es = tok(g.affine_select(T.es[0:32, 0:128], T.s64[0:32, 0:128], [[1, 16], [16, 2], [0, 4]], A.is_equal, 0.0, 0, -1))
+    need(g, t_ones)
+    t_e16 = tok(g.affine_select(T.e16[0:32, 0:64], T.ones[0:32, 0:64], [[1, 16], [0, 4]], A.is_equal, 0.0, 0, -1))
+
+    need(PE, t_ones, t_cc)
+    PE.matmul(T.pss[:, 0:128], T.ones[0:1, 0:128], T.cc[0:1, 0:128], True, False)
+
+    need(V, t_pa, t_pb, t_cn0, t_cn1)
+    t_e = tok(V.tensor_tensor(T.eb[0:16, 0:32], T.cn[0:16, 0:32], T.par2[0:16, 0:32], A.subtract))
+    need(V, t_e)
+    t_v = tok(V.tensor_scalar(T.vb[0:16, 0:32], T.eb[0:16, 0:32], 255, None, A.bitwise_and))
+    need(V, t_v, t_sg0, t_sg1, t_pr0, t_pr1)
+    t_p = tok(V.tensor_tensor(T.pre[0:16, 0:32], T.vb[0:16, 0:32], T.sg[0:16, 0:32], A.mult))
+    need(V, t_p)
+    t_ft = tok(V.transpose(T.ft[0:32, 0:32], T.pre[0:32, 0:32]))
+    need(V, t_ft)
+    t_red = tok(V.tensor_reduce(T.red[0:32, 0:1], T.ft[0:32, 0:32], AxisListType.X, A.min))
+    need(V, t_red, t_dl)
+    t_l2 = tok(V.tensor_scalar(T.l2[0:32, 0:128], T.ones[0:32, 0:128], T.red[0:32, 0:1], T.dl[0:32, 0:1], A.mult, A.add))
+    need(PE, t_l2, t_es)
+    t_pss = tok(PE.matmul(T.pss[:, 0:128], T.l2[0:32, 0:128], T.es[0:32, 0:128], False, True))
+    need(V, t_pss, t_qm)
+    t_offs = tok(V.tensor_scalar(T.offs[:, 0:128], T.pss[:, 0:128], T.qm[:, 0:1], None, A.add))
+    need(V, t_offs, t_c)
+
+    def gather(out, d0, d1):
+        return tok(V.tensor_copy(out, T.cbuf[:, 0:1024].indirect(T.offs[:, 8 * d0:8 * d1])))
+
+    def chunk(h):
+        return gather(T.pack[:, W * base[h]:W * (base[h] + 4)], base[h], base[h] + 4)
+
+    t_gd = chunk(dgn)
+    t_gc = chunk(cb)
+    t_gs = chunk(sw)
+    t_go = []
+    b0 = base[topo.host(core)]
+    if rank > b0:
+        t_go.append(gather(T.pack[:, W * b0:W * rank], b0, rank))
+    if rank < b0 + 3:
+        t_go.append(gather(T.pack[:, W * (rank + 1):W * (b0 + 4)], rank + 1, b0 + 4))
+    t_own = gather(T.land[:, W * rank:W * (rank + 1)], rank, rank + 1)
+
+    sent = 0
+    need(g, t_gd)
+    rl = relay_of(core)
+    rid, pid = topo.addr(rl, core)
+    g.remote_dma(T.rbuf[:, :], T.pack[:, W * base[dgn]:W * (base[dgn] + 4)], T.sem.arr if False else T.sem.rin,
+                 T.sem.snt, pid, rid, msk(eo))
+    sent += len(eo)
+
+    def spread(dsts, engines, per, src_of, dst_ap):
+        trs = []
+        for k, d in enumerate(dsts):
+            trs.append(RemoteDMATransfer(dst_ids=[did(d)], dma_engine_mask=msk(engines[per * k:per * (k + 1)]),
+                                         remote_sem=T.sem.arr, src=src_of(k, d), dst=dst_ap))
+        g.remote_dma_fused(trs, local_sem=T.sem.snt)
+        return per * len(dsts)
+
+    mineland = T.land[:, W * rank:W * (rank + 1)]
+
+    def frompack(k, d):
+        return T.pack[:, W * T.rank_of(d):W * (T.rank_of(d) + 1)]
+
+    need(g, t_gc)
+    sent += spread(byhost[cb], eo, 2, frompack, mineland)
+    need(g, t_gs)
+    sent += spread(byhost[sw], eo, 2, frompack, mineland)
+    need(g, *t_go)
+    sent += spread(peers, eon, 2, frompack, mineland)
+
+    srcs = [x for x in cores if relay_of(x) == core]
+    for x in srcs:
+        g.wait_ge(T.sem.rin, len(eo))
+        rx = T.rank_of(x)
+        sent += spread(byhost[kinds(x)[2]], eo, 2, lambda k, d: T.rbuf[:, W * k:W * (k + 1)],
+                       T.land[:, W * rx:W * (rx + 1)])
+
+    pc = T.par2[0:16, rank:rank + 1]
+    t_parf = tok(V.tensor_copy(T.parf[0:16, 0:1], pc))
+    t_lo = tok(V.tensor_scalar(T.lo[0:16, 0:1], pc, 240, None, A.bitwise_and))
+    need(V, t_parf, t_lo, t_e16)
+    t_lof = tok(V.tensor_copy(T.lof[0:16, 0:1], T.lo[0:16, 0:1]))
+    t_lo8 = tok(V.tensor_scalar(T.lo8[0:16, 0:1], T.lo[0:16, 0:1], 8, None, A.mult))
+    t_dg = tok(V.tensor_scalar(T.dg[0:16, 0:64], T.e16[0:16, 0:64], T.parf[0:16, 0:1], None, A.mult))
+    need(PE, t_dg)
+    t_psm = tok(PE.matmul(T.psm[0:16, 0:64], T.ones[0:16, 0:16], T.dg[0:16, 0:64], True, True))
+    need(V, t_psm, t_lof, t_lo8)
+    t_am = tok(V.tensor_scalar(T.am[0:16, 0:64], T.psm[0:16, 0:64], T.parf[0:16, 0:1], None, A.is_lt))
+    t_bm = tok(V.tensor_scalar(T.bm[0:16, 0:64], T.psm[0:16, 0:64], T.lof[0:16, 0:1], None, A.is_lt))
+    need(V, t_am, t_bm)
+    t_dm = tok(V.tensor_tensor(T.dm[0:16, 0:64], T.am[0:16, 0:64], T.bm[0:16, 0:64], A.subtract))
+    need(V, t_dm)
+    t_ks = tok(V.tensor_reduce(T.ks[0:16, 0:1], T.dm[0:16, 0:64], AxisListType.X, A.add))
+    need(V, t_ks)
+    t_pos = tok(V.tensor_scalar(T.pos[0:16, 0:1], T.ks[0:16, 0:1], 16.0, T.lo8[0:16, 0:1], A.mult, A.add))
+    need(V, t_pos)
+    t_lr = tok(V.tensor_scalar(T.lr[0:16, 0:128], T.ones[0:16, 0:128], T.pos[0:16, 0:1], None, A.mult))
+    need(PE, t_lr, t_e16)
+    PE.matmul(T.psr[:, 0:64], T.ones[0:1, 0:128], T.cc[0:1, 0:64], True, False)
+    t_psr = tok(PE.matmul(T.psr[:, 0:64], T.lr[0:16, 0:128], T.e16[0:16, 0:64], False, True))
+    need(V, t_psr)
+    t_offr = tok(V.tensor_scalar(T.offr[:, 0:64], T.psr[:, 0:64], T.qm[:, 0:1], None, A.add))
+
+    need(V, t_offr, t_own)
+    V.wait_ge(T.sem.arr, 2 * (len(cores) - 1))
+    t_y0 = tok(V.tensor_copy(T.ybuf[:, 0:512], T.land[:, 0:2048].indirect(T.offr[:, 0:32])))
+    t_y1 = tok(V.tensor_copy(T.ybuf[:, 512:1024], T.land[:, 0:2048].indirect(T.offr[:, 32:64])))
+    need(SY, t_y0)
+    t_s0 = tok(SY.dma_start(T.y[:, 0:512], T.ybuf[:, 0:512]), 16)
+    need(AC, t_y1)
+    t_s1 = tok(AC.dma_start(T.y[:, 512:1024], T.ybuf[:, 512:1024]), 16)
+    g.wait_ge(T.sem.snt, sent)
+    need(g, t_s0, t_s1)

@@ -1,5 +1,5 @@
 from concourse.bass import DstId, RemoteDMATransfer
-from concourse.mybir import AluOpType, AxisListType
+from concourse.mybir import AluOpType, AxisListType, ActivationFunctionType
 
 SCRATCH = {
     "cbuf": ("sbuf", [128, 1024], "bfloat16"),
@@ -42,16 +42,38 @@ SCRATCH = {
     "psm": ("psum", [128, 512], "float32"),
     "psr": ("psum", [128, 512], "float32"),
 }
-SEMAPHORES = ["arr", "rin", "snt"] + ["q%d" % i for i in range(64)]
+SEMAPHORES = ["arr", "rin", "snt", "hin"] + ["q%d" % i for i in range(64)]
 
 W = 128
+WORLD = 512
 A = AluOpType
 
 
 def rank_program(g, core, T, topo):
-    rank = T.rank_of(core)
-    if rank is None:
+    cores = list(T.cores)
+
+    def samechip(a, b):
+        return topo.host(a) == topo.host(b) and topo.chip(a) == topo.chip(b)
+
+    near = [x for x in cores if samechip(x, core)]
+    if not near:
         return
+    onchip = [y for y in range(WORLD) if samechip(y, core)]
+
+    def helper_of(x):
+        rk = [y for y in near if topo.die(y) == topo.die(x)]
+        fr = [y for y in onchip if y not in cores and topo.die(y) == topo.die(x)]
+        return fr[rk.index(x)]
+
+    if core in cores:
+        me = core
+    else:
+        owners = [x for x in near if helper_of(x) == core]
+        if not owners:
+            return
+        me = owners[0]
+    rank = T.rank_of(me)
+
     V, PE, SY, AC = g.vector, g.tensor, g.sync, g.scalar
     pool = [0]
 
@@ -65,7 +87,6 @@ def rank_program(g, core, T, topo):
         for s, n in toks:
             q.wait_ge(s, n)
 
-    cores = list(T.cores)
     byhost = {}
     for x in cores:
         byhost.setdefault(topo.host(x), []).append(x)
@@ -103,12 +124,50 @@ def rank_program(g, core, T, topo):
         rid, pid = topo.addr(d, core)
         return DstId(rid=rid, pnc=pid)
 
-    sw, cb, dgn = kinds(core)
-    mine = byhost[topo.host(core)]
-    peers = [x for x in mine if x != core]
+    sw, cb, dgn = kinds(me)
+    mine = byhost[topo.host(me)]
+    peers = [x for x in mine if x != me]
     eo = bits(topo.mask(core, byhost[sw][0]))
     eon = [e for e in bits(topo.mask(core, peers[0])) if e not in eo]
     base = {h: min(T.rank_of(x) for x in lst) for h, lst in byhost.items()}
+
+    def gather(q, out, d0, d1):
+        src = T.cbuf[:, 0:1024].indirect(T.offs[:, 8 * d0:8 * d1])
+        if q is V:
+            return tok(V.tensor_copy(out, src))
+        return tok(AC.activation(out, src, ActivationFunctionType.Copy))
+
+    def topack(q, d0, d1):
+        return gather(q, T.pack[:, W * d0:W * d1], d0, d1)
+
+    def fused(items):
+        trs = [RemoteDMATransfer(dst_ids=[did(d)], dma_engine_mask=msk(es), remote_sem=T.sem.arr, src=s, dst=o)
+               for d, es, s, o in items]
+        g.remote_dma_fused(trs, local_sem=T.sem.snt)
+        return sum(len(es) for _, es, _, _ in items)
+
+    mineland = T.land[:, W * rank:W * (rank + 1)]
+
+    def frompack(d):
+        return T.pack[:, W * T.rank_of(d):W * (T.rank_of(d) + 1)]
+
+    def direct(part):
+        items = []
+        for k in range(2):
+            dc, ds = byhost[cb][2 * part + k], byhost[sw][2 * part + k]
+            items.append((dc, [eo[4 * k], eo[4 * k + 2]], frompack(dc), mineland))
+            items.append((ds, [eo[4 * k + 1], eo[4 * k + 3]], frompack(ds), mineland))
+        return items
+
+    if core != me:
+        V.wait_ge(T.sem.hin, 2 * len(eon))
+        AC.wait_ge(T.sem.hin, 2 * len(eon))
+        t_hc = topack(V, base[cb] + 2, base[cb] + 4)
+        t_hs = topack(AC, base[sw] + 2, base[sw] + 4)
+        need(g, t_hc, t_hs)
+        n = fused(direct(1))
+        g.wait_ge(T.sem.snt, n)
+        return
 
     t_c = tok(SY.dma_start(T.cbuf[:, :], T.c[:, :]), 16)
     t_pa = tok(AC.dma_start(T.par2[0:16, 0:16], T.parent[:, :]), 16)
@@ -139,6 +198,13 @@ def rank_program(g, core, T, topo):
     need(g, t_ones)
     t_e16 = tok(g.affine_select(T.e16[0:32, 0:64], T.ones[0:32, 0:64], [[1, 16], [0, 4]], A.is_equal, 0.0, 0, -1))
 
+    sent = 0
+    hp = helper_of(core)
+    hrid, hpid = topo.addr(hp, core)
+    need(g, t_c)
+    g.remote_dma(T.cbuf[:, :], T.cbuf[:, :], T.sem.hin, T.sem.snt, hpid, hrid, msk(eon))
+    sent += len(eon)
+
     need(PE, t_ones, t_cc)
     PE.matmul(T.pss[:, 0:128], T.ones[0:1, 0:128], T.cc[0:1, 0:128], True, False)
 
@@ -159,58 +225,38 @@ def rank_program(g, core, T, topo):
     need(V, t_pss, t_qm)
     t_offs = tok(V.tensor_scalar(T.offs[:, 0:128], T.pss[:, 0:128], T.qm[:, 0:1], None, A.add))
     need(V, t_offs, t_c)
+    need(AC, t_offs, t_c)
 
-    def gather(out, d0, d1):
-        return tok(V.tensor_copy(out, T.cbuf[:, 0:1024].indirect(T.offs[:, 8 * d0:8 * d1])))
-
-    def chunk(h):
-        return gather(T.pack[:, W * base[h]:W * (base[h] + 4)], base[h], base[h] + 4)
-
-    t_gd = chunk(dgn)
-    t_gc = chunk(cb)
-    t_gs = chunk(sw)
+    t_d0 = topack(V, base[dgn], base[dgn] + 2)
+    t_d1 = topack(AC, base[dgn] + 2, base[dgn] + 4)
+    t_xc = topack(V, base[cb], base[cb] + 2)
+    t_xs = topack(AC, base[sw], base[sw] + 2)
     t_go = []
     b0 = base[topo.host(core)]
     if rank > b0:
-        t_go.append(gather(T.pack[:, W * b0:W * rank], b0, rank))
+        t_go.append(topack(AC, b0, rank))
     if rank < b0 + 3:
-        t_go.append(gather(T.pack[:, W * (rank + 1):W * (b0 + 4)], rank + 1, b0 + 4))
-    t_own = gather(T.land[:, W * rank:W * (rank + 1)], rank, rank + 1)
+        t_go.append(topack(AC, rank + 1, b0 + 4))
+    t_own = gather(V, mineland, rank, rank + 1)
 
-    sent = 0
-    need(g, t_gd)
-    rl = relay_of(core)
-    rid, pid = topo.addr(rl, core)
-    g.remote_dma(T.rbuf[:, :], T.pack[:, W * base[dgn]:W * (base[dgn] + 4)], T.sem.arr if False else T.sem.rin,
-                 T.sem.snt, pid, rid, msk(eo))
+    need(g, t_d0, t_d1)
+    rid, pid = topo.addr(relay_of(core), core)
+    g.remote_dma(T.rbuf[:, :], T.pack[:, W * base[dgn]:W * (base[dgn] + 4)], T.sem.rin, T.sem.snt, pid, rid, msk(eo))
     sent += len(eo)
 
-    def spread(dsts, engines, per, src_of, dst_ap):
-        trs = []
-        for k, d in enumerate(dsts):
-            trs.append(RemoteDMATransfer(dst_ids=[did(d)], dma_engine_mask=msk(engines[per * k:per * (k + 1)]),
-                                         remote_sem=T.sem.arr, src=src_of(k, d), dst=dst_ap))
-        g.remote_dma_fused(trs, local_sem=T.sem.snt)
-        return per * len(dsts)
+    need(g, t_offs)
+    g.remote_dma(T.offs[:, :], T.offs[:, :], T.sem.hin, T.sem.snt, hpid, hrid, msk(eon))
+    sent += len(eon)
 
-    mineland = T.land[:, W * rank:W * (rank + 1)]
-
-    def frompack(k, d):
-        return T.pack[:, W * T.rank_of(d):W * (T.rank_of(d) + 1)]
-
-    need(g, t_gc)
-    sent += spread(byhost[cb], eo, 2, frompack, mineland)
-    need(g, t_gs)
-    sent += spread(byhost[sw], eo, 2, frompack, mineland)
-    need(g, *t_go)
-    sent += spread(peers, eon, 2, frompack, mineland)
+    need(g, t_xc, t_xs, *t_go)
+    sent += fused(direct(0) + [(d, eon[2 * k:2 * k + 2], frompack(d), mineland) for k, d in enumerate(peers)])
 
     srcs = [x for x in cores if relay_of(x) == core]
     for x in srcs:
         g.wait_ge(T.sem.rin, len(eo))
         rx = T.rank_of(x)
-        sent += spread(byhost[kinds(x)[2]], eo, 2, lambda k, d: T.rbuf[:, W * k:W * (k + 1)],
-                       T.land[:, W * rx:W * (rx + 1)])
+        sent += fused([(d, eo[2 * k:2 * k + 2], T.rbuf[:, W * k:W * (k + 1)], T.land[:, W * rx:W * (rx + 1)])
+                       for k, d in enumerate(byhost[kinds(x)[2]])])
 
     pc = T.par2[0:16, rank:rank + 1]
     t_parf = tok(V.tensor_copy(T.parf[0:16, 0:1], pc))
@@ -239,9 +285,12 @@ def rank_program(g, core, T, topo):
     t_offr = tok(V.tensor_scalar(T.offr[:, 0:64], T.psr[:, 0:64], T.qm[:, 0:1], None, A.add))
 
     need(V, t_offr, t_own)
+    need(AC, t_offr, t_own)
     V.wait_ge(T.sem.arr, 2 * (len(cores) - 1))
+    AC.wait_ge(T.sem.arr, 2 * (len(cores) - 1))
     t_y0 = tok(V.tensor_copy(T.ybuf[:, 0:512], T.land[:, 0:2048].indirect(T.offr[:, 0:32])))
-    t_y1 = tok(V.tensor_copy(T.ybuf[:, 512:1024], T.land[:, 0:2048].indirect(T.offr[:, 32:64])))
+    t_y1 = tok(AC.activation(T.ybuf[:, 512:1024], T.land[:, 0:2048].indirect(T.offr[:, 32:64]),
+                             ActivationFunctionType.Copy))
     need(SY, t_y0)
     t_s0 = tok(SY.dma_start(T.y[:, 0:512], T.ybuf[:, 0:512]), 16)
     need(AC, t_y1)

@@ -42,7 +42,7 @@ SCRATCH = {
     "psm": ("psum", [128, 512], "float32"),
     "psr": ("psum", [128, 512], "float32"),
 }
-SEMAPHORES = ["arr", "rin", "snt", "hin"] + ["q%d" % i for i in range(64)]
+SEMAPHORES = ["arr", "rin0", "rin1", "snt", "hin", "hpa"] + ["q%d" % i for i in range(80)]
 
 W = 128
 WORLD = 512
@@ -128,7 +128,8 @@ def rank_program(g, core, T, topo):
     mine = byhost[topo.host(me)]
     peers = [x for x in mine if x != me]
     eo = bits(topo.mask(core, byhost[sw][0]))
-    eon = [e for e in bits(topo.mask(core, peers[0])) if e not in eo]
+    eall = bits(topo.mask(core, peers[0]))
+    eon = [e for e in eall if e not in eo]
     base = {h: min(T.rank_of(x) for x in lst) for h, lst in byhost.items()}
 
     def gather(q, out, d0, d1):
@@ -159,19 +160,16 @@ def rank_program(g, core, T, topo):
             items.append((ds, [eo[4 * k + 1], eo[4 * k + 3]], frompack(ds), mineland))
         return items
 
-    if core != me:
-        V.wait_ge(T.sem.hin, 2 * len(eon))
-        AC.wait_ge(T.sem.hin, 2 * len(eon))
-        t_hc = topack(V, base[cb] + 2, base[cb] + 4)
-        t_hs = topack(AC, base[sw] + 2, base[sw] + 4)
-        need(g, t_hc, t_hs)
-        n = fused(direct(1))
-        g.wait_ge(T.sem.snt, n)
-        return
-
-    t_c = tok(SY.dma_start(T.cbuf[:, :], T.c[:, :]), 16)
-    t_pa = tok(AC.dma_start(T.par2[0:16, 0:16], T.parent[:, :]), 16)
-    t_pb = tok(AC.dma_start(T.par2[0:16, 16:32], T.parent[:, :]), 16)
+    isrank = core == me
+    if isrank:
+        t_pa = tok(SY.dma_start(T.par2[0:16, 0:16], T.parent[:, :]), 16)
+        t_pb = tok(AC.dma_start(T.par2[0:16, 16:32], T.parent[:, :]), 16)
+        t_pc = tok(SY.dma_start(T.par2[16:32, 0:16], T.parent[:, :]), 16)
+        t_pd = tok(AC.dma_start(T.par2[16:32, 16:32], T.parent[:, :]), 16)
+        t_c = tok(SY.dma_start(T.cbuf[:, :], T.c[:, :]), 16)
+        got_par, got_c = [t_pa, t_pb], t_c
+    else:
+        got_par, got_c = [(T.sem.hpa, len(eall))], (T.sem.hin, len(eon))
 
     t_qi = tok(g.iota(T.qi[:, 0:1], [[0, 1]], 0, 1))
     t_cc = tok(g.iota(T.cc[0:1, 0:128], [[0, 32], [16, 4]], 0, 0, allow_small_or_imprecise_dtypes=True))
@@ -179,6 +177,9 @@ def rank_program(g, core, T, topo):
     t_s64a = tok(V.memset(T.s64[0:32, 0:128], -64.0))
     t_dla = tok(V.memset(T.dl[0:32, 0:1], -15.0))
     t_ones = tok(V.memset(T.ones[0:32, 0:128], 1.0))
+    if isrank:
+        t_m1 = tok(V.memset(T.par2[32:64, 0:32], 0))
+        t_m2 = tok(V.memset(T.par2[64:128, 0:32], 0))
     need(V, t_s64a, t_dla)
     t_s64 = tok(V.memset(T.s64[0:16, 0:128], 64.0))
     t_dl = tok(V.memset(T.dl[0:16, 0:1], 255.0))
@@ -195,20 +196,23 @@ def rank_program(g, core, T, topo):
 
     need(g, t_s64)
     t_es = tok(g.affine_select(T.es[0:32, 0:128], T.s64[0:32, 0:128], [[1, 16], [16, 2], [0, 4]], A.is_equal, 0.0, 0, -1))
-    need(g, t_ones)
-    t_e16 = tok(g.affine_select(T.e16[0:32, 0:64], T.ones[0:32, 0:64], [[1, 16], [0, 4]], A.is_equal, 0.0, 0, -1))
 
     sent = 0
-    hp = helper_of(core)
-    hrid, hpid = topo.addr(hp, core)
-    need(g, t_c)
-    g.remote_dma(T.cbuf[:, :], T.cbuf[:, :], T.sem.hin, T.sem.snt, hpid, hrid, msk(eon))
-    sent += len(eon)
+    if isrank:
+        hp = helper_of(core)
+        hrid, hpid = topo.addr(hp, core)
+        need(g, t_pa, t_pb, t_pc, t_pd, t_m1, t_m2)
+        g.remote_dma(T.par2[:, :], T.par2[:, :], T.sem.hpa, T.sem.snt, hpid, hrid, msk(eall))
+        sent += len(eall)
+        need(g, t_c)
+        g.remote_dma(T.cbuf[:, :], T.cbuf[:, :], T.sem.hin, T.sem.snt, hpid, hrid, msk(eon))
+        sent += len(eon)
 
     need(PE, t_ones, t_cc)
     PE.matmul(T.pss[:, 0:128], T.ones[0:1, 0:128], T.cc[0:1, 0:128], True, False)
 
-    need(V, t_pa, t_pb, t_cn0, t_cn1)
+    need(V, *got_par)
+    need(V, t_cn0, t_cn1)
     t_e = tok(V.tensor_tensor(T.eb[0:16, 0:32], T.cn[0:16, 0:32], T.par2[0:16, 0:32], A.subtract))
     need(V, t_e)
     t_v = tok(V.tensor_scalar(T.vb[0:16, 0:32], T.eb[0:16, 0:32], 255, None, A.bitwise_and))
@@ -224,11 +228,19 @@ def rank_program(g, core, T, topo):
     t_pss = tok(PE.matmul(T.pss[:, 0:128], T.l2[0:32, 0:128], T.es[0:32, 0:128], False, True))
     need(V, t_pss, t_qm)
     t_offs = tok(V.tensor_scalar(T.offs[:, 0:128], T.pss[:, 0:128], T.qm[:, 0:1], None, A.add))
-    need(V, t_offs, t_c)
-    need(AC, t_offs, t_c)
+    need(V, t_offs, got_c)
+    need(AC, t_offs, got_c)
 
-    t_d0 = topack(V, base[dgn], base[dgn] + 2)
-    t_d1 = topack(AC, base[dgn] + 2, base[dgn] + 4)
+    if not isrank:
+        t_hc = topack(V, base[cb] + 2, base[cb] + 4)
+        t_hs = topack(AC, base[sw] + 2, base[sw] + 4)
+        need(g, t_hc, t_hs)
+        n = fused(direct(1))
+        g.wait_ge(T.sem.snt, n)
+        return
+
+    dd = base[dgn]
+    t_half = [(topack(V, dd + 2 * h, dd + 2 * h + 1), topack(AC, dd + 2 * h + 1, dd + 2 * h + 2)) for h in range(2)]
     t_xc = topack(V, base[cb], base[cb] + 2)
     t_xs = topack(AC, base[sw], base[sw] + 2)
     t_go = []
@@ -239,24 +251,30 @@ def rank_program(g, core, T, topo):
         t_go.append(topack(AC, rank + 1, b0 + 4))
     t_own = gather(V, mineland, rank, rank + 1)
 
-    need(g, t_d0, t_d1)
     rid, pid = topo.addr(relay_of(core), core)
-    g.remote_dma(T.rbuf[:, :], T.pack[:, W * base[dgn]:W * (base[dgn] + 4)], T.sem.rin, T.sem.snt, pid, rid, msk(eo))
-    sent += len(eo)
+    for h in range(2):
+        need(g, *t_half[h])
+        g.remote_dma(T.rbuf[:, 2 * W * h:2 * W * (h + 1)], T.pack[:, W * (dd + 2 * h):W * (dd + 2 * h + 2)],
+                     T.sem["rin%d" % h], T.sem.snt, pid, rid, msk(eo))
+        sent += len(eo)
 
-    need(g, t_offs)
-    g.remote_dma(T.offs[:, :], T.offs[:, :], T.sem.hin, T.sem.snt, hpid, hrid, msk(eon))
-    sent += len(eon)
+    need(g, t_xc, t_xs)
+    sent += fused(direct(0))
+    need(g, *t_go)
+    sent += fused([(d, eon[2 * k:2 * k + 2], frompack(d), mineland) for k, d in enumerate(peers)])
 
-    need(g, t_xc, t_xs, *t_go)
-    sent += fused(direct(0) + [(d, eon[2 * k:2 * k + 2], frompack(d), mineland) for k, d in enumerate(peers)])
+    need(g, t_ones)
+    t_e16 = tok(g.affine_select(T.e16[0:32, 0:64], T.ones[0:32, 0:64], [[1, 16], [0, 4]], A.is_equal, 0.0, 0, -1))
 
     srcs = [x for x in cores if relay_of(x) == core]
+    nh = len(eo) // 2
     for x in srcs:
-        g.wait_ge(T.sem.rin, len(eo))
         rx = T.rank_of(x)
-        sent += fused([(d, eo[2 * k:2 * k + 2], T.rbuf[:, W * k:W * (k + 1)], T.land[:, W * rx:W * (rx + 1)])
-                       for k, d in enumerate(byhost[kinds(x)[2]])])
+        far = byhost[kinds(x)[2]]
+        for h in range(2):
+            g.wait_ge(T.sem["rin%d" % h], len(eo))
+            sent += fused([(far[2 * h + k], eo[nh * k:nh * (k + 1)], T.rbuf[:, W * (2 * h + k):W * (2 * h + k + 1)],
+                            T.land[:, W * rx:W * (rx + 1)]) for k in range(2)])
 
     pc = T.par2[0:16, rank:rank + 1]
     t_parf = tok(V.tensor_copy(T.parf[0:16, 0:1], pc))
@@ -284,16 +302,16 @@ def rank_program(g, core, T, topo):
     need(V, t_psr)
     t_offr = tok(V.tensor_scalar(T.offr[:, 0:64], T.psr[:, 0:64], T.qm[:, 0:1], None, A.add))
 
+    nfar = len(byhost[dgn])
+    landed = 2 * (len(cores) - 1 - nfar) + nh * nfar
     need(V, t_offr, t_own)
     need(AC, t_offr, t_own)
-    V.wait_ge(T.sem.arr, 2 * (len(cores) - 1))
-    AC.wait_ge(T.sem.arr, 2 * (len(cores) - 1))
+    V.wait_ge(T.sem.arr, landed)
+    AC.wait_ge(T.sem.arr, landed)
     t_y0 = tok(V.tensor_copy(T.ybuf[:, 0:512], T.land[:, 0:2048].indirect(T.offr[:, 0:32])))
     t_y1 = tok(AC.activation(T.ybuf[:, 512:1024], T.land[:, 0:2048].indirect(T.offr[:, 32:64]),
                              ActivationFunctionType.Copy))
-    need(SY, t_y0)
-    t_s0 = tok(SY.dma_start(T.y[:, 0:512], T.ybuf[:, 0:512]), 16)
-    need(AC, t_y1)
-    t_s1 = tok(AC.dma_start(T.y[:, 512:1024], T.ybuf[:, 512:1024]), 16)
+    need(SY, t_y0, t_y1)
+    t_s = tok(SY.dma_start(T.y[:, :], T.ybuf[:, :]), 16)
     g.wait_ge(T.sem.snt, sent)
-    need(g, t_s0, t_s1)
+    need(g, t_s)

from concourse.bass import DstId, RemoteDMATransfer
from concourse.mybir import AluOpType, AxisListType, ActivationFunctionType

SCRATCH = {
    "cbuf": ("sbuf", [128, 1024], "bfloat16"),
    "pack": ("sbuf", [128, 2048], "bfloat16"),
    "land": ("sbuf", [128, 2048], "bfloat16"),
    "rbuf": ("sbuf", [128, 512], "bfloat16"),
    "ybuf": ("sbuf", [128, 1024], "bfloat16"),
    "par2": ("sbuf", [128, 32], "int32"),
    "cn": ("sbuf", [128, 32], "int32"),
    "sg": ("sbuf", [128, 32], "int32"),
    "eb": ("sbuf", [128, 32], "int32"),
    "vb": ("sbuf", [128, 32], "int32"),
    "pre": ("sbuf", [128, 32], "float32"),
    "ft": ("sbuf", [128, 32], "float32"),
    "red": ("sbuf", [128, 1], "float32"),
    "dl": ("sbuf", [128, 1], "float32"),
    "ones": ("sbuf", [128, 128], "bfloat16"),
    "s64": ("sbuf", [128, 128], "bfloat16"),
    "es": ("sbuf", [128, 128], "bfloat16"),
    "e16": ("sbuf", [128, 64], "bfloat16"),
    "l2": ("sbuf", [128, 128], "bfloat16"),
    "cc": ("sbuf", [128, 128], "bfloat16"),
    "qi": ("sbuf", [128, 1], "int32"),
    "qa": ("sbuf", [128, 1], "int32"),
    "qm": ("sbuf", [128, 1], "float32"),
    "offs": ("sbuf", [128, 128], "uint16"),
    "offr": ("sbuf", [128, 64], "uint16"),
    "parf": ("sbuf", [128, 1], "float32"),
    "lo": ("sbuf", [128, 1], "int32"),
    "lof": ("sbuf", [128, 1], "float32"),
    "lo8": ("sbuf", [128, 1], "float32"),
    "dg": ("sbuf", [128, 64], "bfloat16"),
    "am": ("sbuf", [128, 64], "float32"),
    "bm": ("sbuf", [128, 64], "float32"),
    "dm": ("sbuf", [128, 64], "float32"),
    "ks": ("sbuf", [128, 1], "float32"),
    "pos": ("sbuf", [128, 1], "float32"),
    "lr": ("sbuf", [128, 128], "bfloat16"),
    "pss": ("psum", [128, 512], "float32"),
    "psm": ("psum", [128, 512], "float32"),
    "psr": ("psum", [128, 512], "float32"),
}
SEMAPHORES = ["arr", "rin0", "rin1", "snt", "hin", "hpa"] + ["q%d" % i for i in range(80)]

W = 128
WORLD = 512
A = AluOpType


def rank_program(g, core, T, topo):
    cores = list(T.cores)

    def samechip(a, b):
        return topo.host(a) == topo.host(b) and topo.chip(a) == topo.chip(b)

    near = [x for x in cores if samechip(x, core)]
    if not near:
        return
    onchip = [y for y in range(WORLD) if samechip(y, core)]

    def helper_of(x):
        rk = [y for y in near if topo.die(y) == topo.die(x)]
        fr = [y for y in onchip if y not in cores and topo.die(y) == topo.die(x)]
        return fr[rk.index(x)]

    if core in cores:
        me = core
    else:
        owners = [x for x in near if helper_of(x) == core]
        if not owners:
            return
        me = owners[0]
    rank = T.rank_of(me)

    V, PE, SY, AC = g.vector, g.tensor, g.sync, g.scalar
    pool = [0]

    def tok(instr, n=1):
        s = T.sem["q%d" % pool[0]]
        pool[0] += 1
        instr.then_inc(s, n)
        return (s, n)

    def need(q, *toks):
        for s, n in toks:
            q.wait_ge(s, n)

    byhost = {}
    for x in cores:
        byhost.setdefault(topo.host(x), []).append(x)

    def kinds(x):
        sw = cb = dgn = None
        for h, lst in byhost.items():
            if h == topo.host(x):
                continue
            if not topo.may_write(x, lst[0]):
                dgn = h
            elif topo.same_plane(x, lst[0]):
                sw = h
            else:
                cb = h
        return sw, cb, dgn

    def relay_of(x):
        sw, cb, _ = kinds(x)
        mine = byhost[topo.host(x)]
        samedie = [z for z in mine if topo.die(z) == topo.die(x)]
        via = sw if samedie.index(x) % 2 == 0 else cb
        return byhost[via][mine.index(x)]

    def bits(m):
        return [e for e in range(16) if (m >> e) & 1]

    def msk(es):
        m = 0
        for e in es:
            m |= 1 << e
        return m

    def did(d):
        rid, pid = topo.addr(d, core)
        return DstId(rid=rid, pnc=pid)

    sw, cb, dgn = kinds(me)
    mine = byhost[topo.host(me)]
    peers = [x for x in mine if x != me]
    eo = bits(topo.mask(core, byhost[sw][0]))
    eall = bits(topo.mask(core, peers[0]))
    eon = [e for e in eall if e not in eo]
    base = {h: min(T.rank_of(x) for x in lst) for h, lst in byhost.items()}

    def gather(q, out, d0, d1):
        src = T.cbuf[:, 0:1024].indirect(T.offs[:, 8 * d0:8 * d1])
        if q is V:
            return tok(V.tensor_copy(out, src))
        return tok(AC.activation(out, src, ActivationFunctionType.Copy))

    def topack(q, d0, d1):
        return gather(q, T.pack[:, W * d0:W * d1], d0, d1)

    def fused(items):
        trs = [RemoteDMATransfer(dst_ids=[did(d)], dma_engine_mask=msk(es), remote_sem=T.sem.arr, src=s, dst=o)
               for d, es, s, o in items]
        g.remote_dma_fused(trs, local_sem=T.sem.snt)
        return sum(len(es) for _, es, _, _ in items)

    mineland = T.land[:, W * rank:W * (rank + 1)]

    def frompack(d):
        return T.pack[:, W * T.rank_of(d):W * (T.rank_of(d) + 1)]

    def direct(part):
        items = []
        for k in range(2):
            dc, ds = byhost[cb][2 * part + k], byhost[sw][2 * part + k]
            items.append((dc, [eo[4 * k], eo[4 * k + 2]], frompack(dc), mineland))
            items.append((ds, [eo[4 * k + 1], eo[4 * k + 3]], frompack(ds), mineland))
        return items

    isrank = core == me
    if isrank:
        t_pa = tok(SY.dma_start(T.par2[0:16, 0:16], T.parent[:, :]), 16)
        t_pb = tok(AC.dma_start(T.par2[0:16, 16:32], T.parent[:, :]), 16)
        t_pc = tok(SY.dma_start(T.par2[16:32, 0:16], T.parent[:, :]), 16)
        t_pd = tok(AC.dma_start(T.par2[16:32, 16:32], T.parent[:, :]), 16)
        t_c = tok(SY.dma_start(T.cbuf[:, :], T.c[:, :]), 16)
        got_par, got_c = [t_pa, t_pb], t_c
    else:
        got_par, got_c = [(T.sem.hpa, len(eall))], (T.sem.hin, len(eon))

    t_qi = tok(g.iota(T.qi[:, 0:1], [[0, 1]], 0, 1))
    t_cc = tok(g.iota(T.cc[0:1, 0:128], [[0, 32], [16, 4]], 0, 0, allow_small_or_imprecise_dtypes=True))

    t_s64a = tok(V.memset(T.s64[0:32, 0:128], -64.0))
    t_dla = tok(V.memset(T.dl[0:32, 0:1], -15.0))
    t_ones = tok(V.memset(T.ones[0:32, 0:128], 1.0))
    if isrank:
        t_m1 = tok(V.memset(T.par2[32:64, 0:32], 0))
        t_m2 = tok(V.memset(T.par2[64:128, 0:32], 0))
    need(V, t_s64a, t_dla)
    t_s64 = tok(V.memset(T.s64[0:16, 0:128], 64.0))
    t_dl = tok(V.memset(T.dl[0:16, 0:1], 255.0))
    t_cn0 = tok(V.memset(T.cn[0:16, 0:16], 16 * rank + 255))
    t_cn1 = tok(V.memset(T.cn[0:16, 16:32], 16 * rank + 15))
    t_sg0 = tok(V.memset(T.sg[0:16, 0:16], -1))
    t_sg1 = tok(V.memset(T.sg[0:16, 16:32], 1))
    t_pr0 = tok(V.memset(T.pre[0:32, 0:16], -240.0))
    t_pr1 = tok(V.memset(T.pre[0:32, 16:32], 15.0))
    need(V, t_qi)
    t_qa = tok(V.tensor_scalar(T.qa[:, 0:1], T.qi[:, 0:1], 15, None, A.bitwise_and))
    need(V, t_qa)
    t_qm = tok(V.tensor_copy(T.qm[:, 0:1], T.qa[:, 0:1]))

    need(g, t_s64)
    t_es = tok(g.affine_select(T.es[0:32, 0:128], T.s64[0:32, 0:128], [[1, 16], [16, 2], [0, 4]], A.is_equal, 0.0, 0, -1))

    sent = 0
    if isrank:
        hp = helper_of(core)
        hrid, hpid = topo.addr(hp, core)
        need(g, t_pa, t_pb, t_pc, t_pd, t_m1, t_m2)
        g.remote_dma(T.par2[:, :], T.par2[:, :], T.sem.hpa, T.sem.snt, hpid, hrid, msk(eall))
        sent += len(eall)
        need(g, t_c)
        g.remote_dma(T.cbuf[:, :], T.cbuf[:, :], T.sem.hin, T.sem.snt, hpid, hrid, msk(eon))
        sent += len(eon)

    need(PE, t_ones, t_cc)
    PE.matmul(T.pss[:, 0:128], T.ones[0:1, 0:128], T.cc[0:1, 0:128], True, False)

    need(V, *got_par)
    need(V, t_cn0, t_cn1)
    t_e = tok(V.tensor_tensor(T.eb[0:16, 0:32], T.cn[0:16, 0:32], T.par2[0:16, 0:32], A.subtract))
    need(V, t_e)
    t_v = tok(V.tensor_scalar(T.vb[0:16, 0:32], T.eb[0:16, 0:32], 255, None, A.bitwise_and))
    need(V, t_v, t_sg0, t_sg1, t_pr0, t_pr1)
    t_p = tok(V.tensor_tensor(T.pre[0:16, 0:32], T.vb[0:16, 0:32], T.sg[0:16, 0:32], A.mult))
    need(V, t_p)
    t_ft = tok(V.transpose(T.ft[0:32, 0:32], T.pre[0:32, 0:32]))
    need(V, t_ft)
    t_red = tok(V.tensor_reduce(T.red[0:32, 0:1], T.ft[0:32, 0:32], AxisListType.X, A.min))
    need(V, t_red, t_dl)
    t_l2 = tok(V.tensor_scalar(T.l2[0:32, 0:128], T.ones[0:32, 0:128], T.red[0:32, 0:1], T.dl[0:32, 0:1], A.mult, A.add))
    need(PE, t_l2, t_es)
    t_pss = tok(PE.matmul(T.pss[:, 0:128], T.l2[0:32, 0:128], T.es[0:32, 0:128], False, True))
    need(V, t_pss, t_qm)
    t_offs = tok(V.tensor_scalar(T.offs[:, 0:128], T.pss[:, 0:128], T.qm[:, 0:1], None, A.add))
    need(V, t_offs, got_c)
    need(AC, t_offs, got_c)

    if not isrank:
        t_hc = topack(V, base[cb] + 2, base[cb] + 4)
        t_hs = topack(AC, base[sw] + 2, base[sw] + 4)
        need(g, t_hc, t_hs)
        n = fused(direct(1))
        g.wait_ge(T.sem.snt, n)
        return

    dd = base[dgn]
    t_half = [(topack(V, dd + 2 * h, dd + 2 * h + 1), topack(AC, dd + 2 * h + 1, dd + 2 * h + 2)) for h in range(2)]
    t_xc = topack(V, base[cb], base[cb] + 2)
    t_xs = topack(AC, base[sw], base[sw] + 2)
    t_go = []
    b0 = base[topo.host(core)]
    if rank > b0:
        t_go.append(topack(AC, b0, rank))
    if rank < b0 + 3:
        t_go.append(topack(AC, rank + 1, b0 + 4))
    t_own = gather(V, mineland, rank, rank + 1)

    rid, pid = topo.addr(relay_of(core), core)
    for h in range(2):
        need(g, *t_half[h])
        g.remote_dma(T.rbuf[:, 2 * W * h:2 * W * (h + 1)], T.pack[:, W * (dd + 2 * h):W * (dd + 2 * h + 2)],
                     T.sem["rin%d" % h], T.sem.snt, pid, rid, msk(eo))
        sent += len(eo)

    need(g, t_xc, t_xs)
    sent += fused(direct(0))
    need(g, *t_go)
    sent += fused([(d, eon[2 * k:2 * k + 2], frompack(d), mineland) for k, d in enumerate(peers)])

    need(g, t_ones)
    t_e16 = tok(g.affine_select(T.e16[0:32, 0:64], T.ones[0:32, 0:64], [[1, 16], [0, 4]], A.is_equal, 0.0, 0, -1))

    srcs = [x for x in cores if relay_of(x) == core]
    nh = len(eo) // 2
    for x in srcs:
        rx = T.rank_of(x)
        far = byhost[kinds(x)[2]]
        for h in range(2):
            g.wait_ge(T.sem["rin%d" % h], len(eo))
            sent += fused([(far[2 * h + k], eo[nh * k:nh * (k + 1)], T.rbuf[:, W * (2 * h + k):W * (2 * h + k + 1)],
                            T.land[:, W * rx:W * (rx + 1)]) for k in range(2)])

    pc = T.par2[0:16, rank:rank + 1]
    t_parf = tok(V.tensor_copy(T.parf[0:16, 0:1], pc))
    t_lo = tok(V.tensor_scalar(T.lo[0:16, 0:1], pc, 240, None, A.bitwise_and))
    need(V, t_parf, t_lo, t_e16)
    t_lof = tok(V.tensor_copy(T.lof[0:16, 0:1], T.lo[0:16, 0:1]))
    t_lo8 = tok(V.tensor_scalar(T.lo8[0:16, 0:1], T.lo[0:16, 0:1], 8, None, A.mult))
    t_dg = tok(V.tensor_scalar(T.dg[0:16, 0:64], T.e16[0:16, 0:64], T.parf[0:16, 0:1], None, A.mult))
    need(PE, t_dg)
    t_psm = tok(PE.matmul(T.psm[0:16, 0:64], T.ones[0:16, 0:16], T.dg[0:16, 0:64], True, True))
    need(V, t_psm, t_lof, t_lo8)
    t_am = tok(V.tensor_scalar(T.am[0:16, 0:64], T.psm[0:16, 0:64], T.parf[0:16, 0:1], None, A.is_lt))
    t_bm = tok(V.tensor_scalar(T.bm[0:16, 0:64], T.psm[0:16, 0:64], T.lof[0:16, 0:1], None, A.is_lt))
    need(V, t_am, t_bm)
    t_dm = tok(V.tensor_tensor(T.dm[0:16, 0:64], T.am[0:16, 0:64], T.bm[0:16, 0:64], A.subtract))
    need(V, t_dm)
    t_ks = tok(V.tensor_reduce(T.ks[0:16, 0:1], T.dm[0:16, 0:64], AxisListType.X, A.add))
    need(V, t_ks)
    t_pos = tok(V.tensor_scalar(T.pos[0:16, 0:1], T.ks[0:16, 0:1], 16.0, T.lo8[0:16, 0:1], A.mult, A.add))
    need(V, t_pos)
    t_lr = tok(V.tensor_scalar(T.lr[0:16, 0:128], T.ones[0:16, 0:128], T.pos[0:16, 0:1], None, A.mult))
    need(PE, t_lr, t_e16)
    PE.matmul(T.psr[:, 0:64], T.ones[0:1, 0:128], T.cc[0:1, 0:64], True, False)
    t_psr = tok(PE.matmul(T.psr[:, 0:64], T.lr[0:16, 0:128], T.e16[0:16, 0:64], False, True))
    need(V, t_psr)
    t_offr = tok(V.tensor_scalar(T.offr[:, 0:64], T.psr[:, 0:64], T.qm[:, 0:1], None, A.add))

    nfar = len(byhost[dgn])
    landed = 2 * (len(cores) - 1 - nfar) + nh * nfar
    need(V, t_offr, t_own)
    need(AC, t_offr, t_own)
    V.wait_ge(T.sem.arr, landed)
    AC.wait_ge(T.sem.arr, landed)
    t_y0 = tok(V.tensor_copy(T.ybuf[:, 0:512], T.land[:, 0:2048].indirect(T.offr[:, 0:32])))
    t_y1 = tok(AC.activation(T.ybuf[:, 512:1024], T.land[:, 0:2048].indirect(T.offr[:, 32:64]),
                             ActivationFunctionType.Copy))
    need(SY, t_y0, t_y1)
    t_s = tok(SY.dma_start(T.y[:, :], T.ybuf[:, :]), 16)
    g.wait_ge(T.sem.snt, sent)
    need(g, t_s)
